import numpy as np
import ml_dtypes


def mxq(x, axis, fmt="e4m3"):
    dtype, down = {"e4m3": (ml_dtypes.float8_e4m3fn, 7), "e5m2": (ml_dtypes.float8_e5m2, 14)}[fmt]
    v = np.moveaxis(np.asarray(x, np.float32).astype(ml_dtypes.bfloat16).astype(np.float64), axis, -1)
    blocks = v.reshape(v.shape[:-1] + (-1, 32))
    amax = np.abs(blocks).max(-1, keepdims=True)
    byte = np.maximum(np.where(amax > 0, np.frexp(amax)[1] - 1 + 127, 0) - down, 1)
    scale = np.exp2(byte - 127.0)
    codes = (blocks / scale).astype(np.float32).astype(dtype).astype(np.float64)
    return np.moveaxis((codes * scale).reshape(v.shape), -1, axis)


WIDE = False


def mx_kscale(k):
    if not WIDE:
        return np.ones(k)
    levels = np.array([30, -30])
    if k % 512:
        return np.exp2(np.random.permutation(np.resize(levels, k // 32))).repeat(32)
    a = np.empty((k // 512, 16))
    for p in range(k // 512):
        a[p, :8] = np.random.permutation(np.resize(levels, 8))
        for g in range(8):
            far = levels[np.abs(levels - a[p, g]) >= 10]
            a[p, g + 8] = far[np.random.randint(len(far))]
    return np.exp2(a.ravel()).repeat(32)


def f64(x):
    return np.asarray(x).astype(np.float64)


def striped(idx):
    return np.tile(np.asarray(idx).reshape(-1, 16).T, (8, 1)).astype(np.uint16)


def unstriped(offs):
    return offs[:16].T.reshape(-1).astype(np.int64)


E2M1 = np.array([0.0, 0.5, 1.0, 1.5, 2.0, 3.0, 4.0, 6.0, -0.0, -0.5, -1.0, -1.5, -2.0, -3.0, -4.0, -6.0])


def pack_weight(w, fmt):
    k, n = w.shape
    w = f64(np.asarray(w, np.float32).astype(ml_dtypes.bfloat16)).reshape(k // 32, 32, n)
    amax = np.abs(w).max(1)
    if fmt == "e4m3":
        byte = np.frexp(amax)[1] - 1 + 127 - 7
    else:
        mant, ex = np.frexp(amax / 6.0)
        byte = np.where(mant > 0.5, ex, ex - 1) + 127
    byte = np.clip(np.where(amax > 0, byte, 1), 1, 254)
    scaled = (w * np.exp2(127.0 - byte)[:, None, :]).reshape(k, n).astype(np.float32)
    by_word = np.ascontiguousarray(scaled.reshape(k // 512, 128, 4, n).transpose(0, 1, 3, 2))
    if fmt == "e4m3":
        words = by_word.astype(ml_dtypes.float8_e4m3fn).view(np.uint8)
    else:
        c = by_word.astype(ml_dtypes.float4_e2m1fn).view(np.uint8) & 0xF
        words = (c[..., 0::2] | (c[..., 1::2] << 4)).reshape(k // 512, 128, 2 * n)
    return np.ascontiguousarray(words), np.ascontiguousarray(byte.astype(np.uint8).reshape(k // 512, 16, n))


def unpack_weight(words, scales, fmt):
    g, _, n = scales.shape
    words = np.ascontiguousarray(words).reshape(g, 128, n, -1)
    if fmt == "e4m3":
        vals = words.view(ml_dtypes.float8_e4m3fn).astype(np.float64)
    else:
        nib = np.empty((g, 128, n, 4), np.uint8)
        nib[..., 0::2] = words & 0xF
        nib[..., 1::2] = words >> 4
        vals = E2M1[nib]
    vals = vals * np.repeat(np.exp2(scales.astype(np.float64) - 127.0), 8, axis=1)[..., None]
    return vals.transpose(0, 1, 3, 2).reshape(g * 512, n)


def sigmoid(v):
    return 1.0 / (1.0 + np.exp(-v))


K, F, T, Z, J, R, O, N, E = 512, 512, 1024, 1024, 256, 512, 128, 256, 1024


def setup_inputs():
    n = np.random.standard_normal
    idx = np.random.permutation(T)[:J]
    idx2 = np.random.permutation(Z)[:J]
    idx3 = np.random.permutation(J)[:O]
    idx4 = np.random.permutation(J)[:O]
    idx5 = np.random.permutation(E)[:O]
    fk = mx_kscale(K)
    ff = mx_kscale(F)
    fr = mx_kscale(R)
    xtp = pack_weight(n((K, T)) / fk[:, None], "e2m1")
    wp = pack_weight(n((K, R)) * 1 / np.sqrt(K) * fk[:, None], "e4m3")
    xop = pack_weight(n((F, Z)) / ff[:, None], "e4m3")
    w2p = pack_weight(n((F, R)) * 1 / np.sqrt(F) * ff[:, None] * fr, "e2m1")
    wbp = pack_weight(n((R, N)) * 1 / np.sqrt(R) / fr[:, None], "e2m1")
    return {
        "xt_words": xtp[0],
        "xt_scales": xtp[1],
        "w_words": wp[0],
        "w_scales": wp[1],
        "xo_words": xop[0],
        "xo_scales": xop[1],
        "w2_words": w2p[0],
        "w2_scales": w2p[1],
        "sg": (np.random.uniform(0.6, 1.6, (R, 1))).astype(np.float32),
        "wb_words": wbp[0],
        "wb_scales": wbp[1],
        "tz": (n((N, E))).astype(np.float32),
        "offs": striped(idx),
        "offs2": striped(idx2),
        "offs3": striped(idx3),
        "offs4": striped(idx4),
        "offs5": striped(idx5),
    }


def reference(xt_words, xt_scales, w_words, w_scales, xo_words, xo_scales, w2_words, w2_scales, sg, wb_words, wb_scales, tz, offs, offs2, offs3, offs4, offs5):
    idx = unstriped(offs)
    idx2 = unstriped(offs2)
    idx3 = unstriped(offs3)
    idx4 = unstriped(offs4)
    idx5 = unstriped(offs5)
    xtu = unpack_weight(xt_words, xt_scales, "e2m1")
    wu = unpack_weight(w_words, w_scales, "e4m3")
    xou = unpack_weight(xo_words, xo_scales, "e4m3")
    w2u = unpack_weight(w2_words, w2_scales, "e2m1")
    wbu = unpack_weight(wb_words, wb_scales, "e2m1")
    xtidxg = xtu[:, idx]
    a = wu.T @ xtidxg
    xoidx2g = xou[:, idx2]
    b = w2u.T @ xoidx2g
    hid = np.maximum(b[:, idx3], b[:, idx4]) * sigmoid(a[:, idx4] * f64(sg))
    hidq = mxq(hid, 0, "e5m2")
    p = wbu.T @ hidq
    y = p + f64(tz)[:, idx5]
    return y

@@ -1,0 +1,160 @@
+from contextlib import ExitStack
+
+import concourse.mybir as mybir
+
+F32 = mybir.dt.float32
+BF16 = mybir.dt.bfloat16
+I32 = mybir.dt.int32
+U32 = mybir.dt.uint32
+U16 = mybir.dt.uint16
+U8 = mybir.dt.uint8
+E4M3 = mybir.dt.float8_e4m3fn_x4
+E5M2 = mybir.dt.float8_e5m2_x4
+E2M1 = mybir.dt.float4_e2m1fn_x4
+ACT = mybir.ActivationFunctionType
+ALU = mybir.AluOpType
+
+P = 128
+PACK = 4
+T, Z, J, R, O, N, E = 1024, 1024, 256, 512, 128, 256, 1024
+FLOPS = 2 * 512 * R * J * 2 + 2 * R * N * O
+
+
+def tile_list_twotab_agree_one_tabled_kernel(
+    tc, xt_words, xt_scales, w_words, w_scales, xo_words, xo_scales, w2_words, w2_scales,
+    sg, wb_words, wb_scales, tz, offs, offs2, offs3, offs4, offs5, out,
+):
+    nc = tc.nc
+    with ExitStack() as ctx:
+        sb = ctx.enter_context(tc.tile_pool(name="sb", bufs=1))
+        ps = ctx.enter_context(tc.psum_pool(name="ps", bufs=1))
+
+        def tile(name, shape, dtype, tag=""):
+            return sb.tile(shape, dtype, name=name, tag=tag or name, align_bytes=64)
+
+        def load_list(name, src):
+            dst = tile(name, list(src.shape), U16)
+            nc.sync.dma_start(dst[:], src)
+            return dst
+
+        def load_plane(queues, plane, scales):
+            for q in range(4):
+                rows = scales[0, 4 * q : 4 * q + 4, :].bitcast(I32)
+                queues[q].dma_start(plane[32 * q : 32 * q + 32, :].bitcast(I32), rows.partition_broadcast(8))
+
+        def load_live_rows(queues, plane, scales):
+            for r in range(PACK):
+                queues[r].dma_start(plane[r:P:32, :].bitcast(I32), scales[0, r:16:PACK, :].bitcast(I32))
+
+        xo_plane = tile("xo_plane", [P, Z], U8)
+        xt_plane = tile("xt_plane", [P, T], U8)
+        w2_plane = tile("w2_plane", [P, R], U8)
+        w_plane = tile("w_plane", [P, R], U8)
+        wb_plane = tile("wb_plane", [P, N], U8)
+
+        xo_tab = tile("xo_tab", [P, Z], U32)
+        xt_tab = tile("xt_tab", [P, T], U16)
+        w_raw = tile("w_raw", [P, R], U32)
+        w2_raw = tile("w2_raw", [P, R], U16)
+        wb_codes = tile("wb_codes", [P, N], U16)
+        slope = tile("slope", [P, PACK], F32)
+        tz_tab = tile("tz_tab", [P, 2, E], F32)
+
+        nc.sync.dma_start(xo_tab[:].bitcast(I32), xo_words[0].rearrange("p n t -> p (n t)").bitcast(I32))
+        list2 = load_list("list2", offs2)
+        load_plane([nc.scalar] * 4, xo_plane, xo_scales)
+        nc.sync.dma_start(w2_raw[:].bitcast(I32), w2_words[0].bitcast(I32))
+        load_plane([nc.sync] * 4, w2_plane, w2_scales)
+        nc.sync.dma_start(xt_tab[:].bitcast(I32), xt_words[0].bitcast(I32))
+        list1 = load_list("list1", offs)
+        load_plane([nc.sync] * 4, xt_plane, xt_scales)
+        nc.sync.dma_start(w_raw[:].bitcast(I32), w_words[0].rearrange("p n t -> p (n t)").bitcast(I32))
+        load_plane([nc.sync] * 4, w_plane, w_scales)
+        list3 = load_list("list3", offs3)
+        list4 = load_list("list4", offs4)
+        nc.sync.dma_start(slope[:], sg.rearrange("(p t) o -> p (t o)", t=PACK))
+        list5 = load_list("list5", offs5)
+        nc.sync.dma_start(tz_tab[:], tz.rearrange("(h p) e -> p h e", p=P))
+        nc.sync.dma_start(wb_codes[:].bitcast(I32), wb_words[0].bitcast(I32))
+        load_live_rows([nc.sync] * 4, wb_plane, wb_scales)
+
+        def deal(copy, dst, src):
+            copy(dst[:].rearrange("p (t m) -> p m t", t=PACK), src[:].rearrange("p (m t) -> p m t", t=PACK))
+
+        xo_codes = tile("xo_codes", [P, J], U32)
+        xo_sc = tile("xo_sc", [P, J], U8)
+        nc.vector.tensor_copy(xo_codes[:], xo_tab[:].indirect(list2[:]))
+        nc.vector.tensor_copy(xo_sc[:], xo_plane[:].indirect(list2[:]))
+        w2_codes = tile("w2_codes", [P, R], U16)
+        w2_sc = tile("w2_sc", [P, R], U8)
+        deal(nc.scalar.copy, w2_codes, w2_raw)
+        deal(nc.vector.tensor_copy, w2_sc, w2_plane)
+
+        xt_codes = tile("xt_codes", [P, J], U16)
+        xt_sc = tile("xt_sc", [P, J], U8)
+        nc.vector.tensor_copy(xt_codes[:], xt_tab[:].indirect(list1[:]))
+        nc.vector.tensor_copy(xt_sc[:], xt_plane[:].indirect(list1[:]))
+        w_codes = tile("w_codes", [P, R], U32)
+        w_sc = tile("w_sc", [P, R], U8)
+        deal(nc.scalar.copy, w_codes, w_raw)
+        deal(nc.vector.tensor_copy, w_sc, w_plane)
+
+        b_rows = []
+        for u in range(2):
+            bank = ps.tile([P, 2, J], F32, name="b_bank%d" % u)
+            for v in range(2):
+                cols = slice(P * (2 * u + v), P * (2 * u + v + 1))
+                nc.tensor.matmul_mx(
+                    bank[:, v, :], lhsT=w2_codes[:, cols].bitcast(E2M1), lhsT_scale=w2_sc[:, cols],
+                    rhs=xo_codes[:].bitcast(E4M3), rhs_scale=xo_sc[:], start=True, stop=True,
+                )
+            rows = tile("b_rows%d" % u, [P, 2, J], F32)
+            nc.scalar.copy(rows[:], bank[:])
+            b_rows.append(rows)
+
+        b3 = tile("b3", [P, PACK, O], F32)
+        b4 = tile("b4", [P, PACK, O], F32)
+        top = tile("top", [P, PACK, O], F32)
+        for u in range(2):
+            for v in range(2):
+                nc.vector.tensor_copy(b3[:, 2 * u + v, :], b_rows[u][:, v, :].indirect(list3[:]))
+                nc.scalar.activation(b4[:, 2 * u + v, :], b_rows[u][:, v, :].indirect(list4[:]), ACT.Copy)
+            pair = slice(2 * u, 2 * u + 2)
+            nc.vector.tensor_tensor(top[:, pair, :], b3[:, pair, :], b4[:, pair, :], ALU.max)
+
+        gate = tile("gate", [P, PACK, O], F32)
+        for t in range(PACK):
+            cols = slice(P * t, P * (t + 1))
+            bank = ps.tile([P, J], F32, name="a_bank%d" % t)
+            nc.tensor.matmul_mx(
+                bank[:], lhsT=w_codes[:, cols].bitcast(E4M3), lhsT_scale=w_sc[:, cols],
+                rhs=xt_codes[:].bitcast(E2M1), rhs_scale=xt_sc[:], start=True, stop=True,
+            )
+            rows = tile("a_rows%d" % t, [P, J], F32)
+            nc.vector.tensor_copy(rows[:], bank[:])
+            nc.scalar.activation(gate[:, t, :], rows[:].indirect(list4[:]), ACT.Sigmoid, scale=slope[:, t : t + 1])
+
+        hid = tile("hid", [P, O, PACK], BF16)
+        nc.vector.tensor_tensor(
+            hid[:].rearrange("p (c i) t -> p c t i", i=4),
+            top[:].rearrange("p t (c i) -> p c t i", i=4),
+            gate[:].rearrange("p t (c i) -> p c t i", i=4),
+            ALU.mult,
+        )
+        hid_codes = tile("hid_codes", [P, O], U32)
+        hid_sc = tile("hid_sc", [P, O], U8)
+        nc.vector.quantize_mx(hid_codes[:].bitcast(E5M2), hid_sc[:], hid[:].rearrange("p o t -> p (o t)"))
+
+        tz_picked = tile("tz_picked", [P, 2, O], F32, tag="a_rows3")
+        res = tile("res", [P, 2, O], F32)
+        for h in range(2):
+            nc.scalar.activation(tz_picked[:, h, :], tz_tab[:, h, :].indirect(list5[:]), ACT.Copy)
+        for h, queue in enumerate((nc.sync, nc.scalar)):
+            cols = slice(P * h, P * (h + 1))
+            bank = ps.tile([P, O], F32, name="p_bank%d" % h)
+            nc.tensor.matmul_mx(
+                bank[:], lhsT=wb_codes[:, cols].bitcast(E2M1), lhsT_scale=wb_plane[:, cols],
+                rhs=hid_codes[:].bitcast(E5M2), rhs_scale=hid_sc[:], start=True, stop=True,
+            )
+            nc.vector.tensor_tensor(res[:, h, :], bank[:], tz_picked[:, h, :], ALU.add)
+            queue.dma_start(out[cols, :], res[:, h, :])

@@ -37,20 +37,22 @@ def tile_list_twotab_agree_one_tabled_kernel(
             nc.sync.dma_start(dst[:], src)
             return dst
 
-        def load_plane(queues, plane, scales):
-            for q in range(4):
-                rows = scales[0, 4 * q : 4 * q + 4, :].bitcast(I32)
-                queues[q].dma_start(plane[32 * q : 32 * q + 32, :].bitcast(I32), rows.partition_broadcast(8))
+        def load_rows(queue, name, scales):
+            rows = scales[0].bitcast(I32)
+            words = rows.shape[1]
+            dst = tile(name, [P, 4 * words], U8)
+            queue.dma_start(dst[:].bitcast(I32), rows.unsqueeze(1).to_broadcast([16, 8, words]))
+            return dst
 
-        def load_live_rows(queues, plane, scales):
-            for r in range(PACK):
-                queues[r].dma_start(plane[r:P:32, :].bitcast(I32), scales[0, r:16:PACK, :].bitcast(I32))
+        def compact(planes):
+            words = planes[:].bitcast(I32)
+            for r in range(1, PACK):
+                nc.sync.dma_start(words[r:P:32, :], words[8 * r : P : 32, :])
 
-        xo_plane = tile("xo_plane", [P, Z], U8)
-        xt_plane = tile("xt_plane", [P, T], U8)
-        w2_plane = tile("w2_plane", [P, R], U8)
-        w_plane = tile("w_plane", [P, R], U8)
-        wb_plane = tile("wb_plane", [P, N], U8)
+        b_planes = tile("b_planes", [P, R + J], U8)
+        a_planes = tile("a_planes", [P, R + J + N], U8)
+        w2_sc, xo_sc = b_planes[:, 0:R], b_planes[:, R : R + J]
+        w_sc, xt_sc, wb_plane = a_planes[:, 0:R], a_planes[:, R : R + J], a_planes[:, R + J :]
 
         xo_tab = tile("xo_tab", [P, Z], U32)
         xt_tab = tile("xt_tab", [P, T], U16)
@@ -58,71 +60,77 @@ def tile_list_twotab_agree_one_tabled_kernel(
         w2_raw = tile("w2_raw", [P, R], U16)
         wb_codes = tile("wb_codes", [P, N], U16)
         slope = tile("slope", [P, PACK], F32)
-        tz_tab = tile("tz_tab", [P, 2, E], F32)
 
-        nc.sync.dma_start(xo_tab[:].bitcast(I32), xo_words[0].rearrange("p n t -> p (n t)").bitcast(I32))
+        xo_rows = load_rows(nc.scalar, "xo_rows", xo_scales)
         list2 = load_list("list2", offs2)
-        load_plane([nc.scalar] * 4, xo_plane, xo_scales)
-        nc.sync.dma_start(w2_raw[:].bitcast(I32), w2_words[0].bitcast(I32))
-        load_plane([nc.sync] * 4, w2_plane, w2_scales)
-        nc.sync.dma_start(xt_tab[:].bitcast(I32), xt_words[0].bitcast(I32))
+        w2_rows = load_rows(nc.scalar, "w2_rows", w2_scales)
         list1 = load_list("list1", offs)
-        load_plane([nc.sync] * 4, xt_plane, xt_scales)
-        nc.sync.dma_start(w_raw[:].bitcast(I32), w_words[0].rearrange("p n t -> p (n t)").bitcast(I32))
-        load_plane([nc.sync] * 4, w_plane, w_scales)
+        xt_rows = load_rows(nc.scalar, "xt_rows", xt_scales)
         list3 = load_list("list3", offs3)
+        w_rows = load_rows(nc.scalar, "w_rows", w_scales)
+        nc.sync.dma_start(xo_tab[:].bitcast(I32), xo_words[0].rearrange("p n t -> p (n t)").bitcast(I32))
         list4 = load_list("list4", offs4)
-        nc.sync.dma_start(slope[:], sg.rearrange("(p t) o -> p (t o)", t=PACK))
         list5 = load_list("list5", offs5)
-        nc.sync.dma_start(tz_tab[:], tz.rearrange("(h p) e -> p h e", p=P))
-        nc.sync.dma_start(wb_codes[:].bitcast(I32), wb_words[0].bitcast(I32))
-        load_live_rows([nc.sync] * 4, wb_plane, wb_scales)
+        nc.sync.dma_start(w2_raw[:].bitcast(I32), w2_words[0].bitcast(I32))
+        nc.sync.dma_start(xt_tab[:].bitcast(I32), xt_words[0].bitcast(I32))
+        nc.sync.dma_start(w_raw[:].bitcast(I32), w_words[0].rearrange("p n t -> p (n t)").bitcast(I32))
+        nc.gpsimd.dma_start(wb_plane[0:P:8, :].bitcast(I32), wb_scales[0].bitcast(I32))
+        nc.gpsimd.dma_start(slope[:], sg.rearrange("(p t) o -> p (t o)", t=PACK))
+        nc.gpsimd.dma_start(wb_codes[:].bitcast(I32), wb_words[0].bitcast(I32))
+        warm = tile("warm", [P, 2], F32)
+        nc.vector.memset(warm[:, 0:1], 0.0)
+        nc.scalar.activation(warm[:, 1:2], warm[:, 0:1], ACT.Sigmoid)
 
         def deal(copy, dst, src):
             copy(dst[:].rearrange("p (t m) -> p m t", t=PACK), src[:].rearrange("p (m t) -> p m t", t=PACK))
 
+        xo_picked = tile("xo_picked", [P, J], U8)
+        nc.vector.tensor_copy(xo_picked[:], xo_rows[:].indirect(list2[:]))
+        deal(nc.vector.tensor_copy, w2_sc, w2_rows)
+        nc.vector.tensor_copy(xo_sc.bitcast(I32), xo_picked[:].bitcast(I32))
+        compact(b_planes)
+
+        xt_picked = tile("xt_picked", [P, J], U8)
+        nc.vector.tensor_copy(xt_picked[:], xt_rows[:].indirect(list1[:]))
+        deal(nc.vector.tensor_copy, w_sc, w_rows)
+        nc.vector.tensor_copy(xt_sc.bitcast(I32), xt_picked[:].bitcast(I32))
+        compact(a_planes)
+
         xo_codes = tile("xo_codes", [P, J], U32)
-        xo_sc = tile("xo_sc", [P, J], U8)
         nc.vector.tensor_copy(xo_codes[:], xo_tab[:].indirect(list2[:]))
-        nc.vector.tensor_copy(xo_sc[:], xo_plane[:].indirect(list2[:]))
-        w2_codes = tile("w2_codes", [P, R], U16)
-        w2_sc = tile("w2_sc", [P, R], U8)
-        deal(nc.scalar.copy, w2_codes, w2_raw)
-        deal(nc.vector.tensor_copy, w2_sc, w2_plane)
-
         xt_codes = tile("xt_codes", [P, J], U16)
-        xt_sc = tile("xt_sc", [P, J], U8)
         nc.vector.tensor_copy(xt_codes[:], xt_tab[:].indirect(list1[:]))
-        nc.vector.tensor_copy(xt_sc[:], xt_plane[:].indirect(list1[:]))
+        w2_codes = tile("w2_codes", [P, R], U16)
+        deal(nc.scalar.copy, w2_codes, w2_raw)
         w_codes = tile("w_codes", [P, R], U32)
-        w_sc = tile("w_sc", [P, R], U8)
         deal(nc.scalar.copy, w_codes, w_raw)
-        deal(nc.vector.tensor_copy, w_sc, w_plane)
 
-        b_rows = []
-        for u in range(2):
-            bank = ps.tile([P, 2, J], F32, name="b_bank%d" % u)
-            for v in range(2):
-                cols = slice(P * (2 * u + v), P * (2 * u + v + 1))
-                nc.tensor.matmul_mx(
-                    bank[:, v, :], lhsT=w2_codes[:, cols].bitcast(E2M1), lhsT_scale=w2_sc[:, cols],
-                    rhs=xo_codes[:].bitcast(E4M3), rhs_scale=xo_sc[:], start=True, stop=True,
-                )
-            rows = tile("b_rows%d" % u, [P, 2, J], F32)
-            nc.scalar.copy(rows[:], bank[:])
-            b_rows.append(rows)
+        tz_tab = tile("tz_tab", [P, 2, E], F32, tag="xt_tab")
+        nc.sync.dma_start(tz_tab[:], tz.rearrange("(h p) e -> p h e", p=P))
 
         b3 = tile("b3", [P, PACK, O], F32)
         b4 = tile("b4", [P, PACK, O], F32)
         top = tile("top", [P, PACK, O], F32)
-        for u in range(2):
-            for v in range(2):
-                nc.vector.tensor_copy(b3[:, 2 * u + v, :], b_rows[u][:, v, :].indirect(list3[:]))
-                nc.scalar.activation(b4[:, 2 * u + v, :], b_rows[u][:, v, :].indirect(list4[:]), ACT.Copy)
-            pair = slice(2 * u, 2 * u + 2)
-            nc.vector.tensor_tensor(top[:, pair, :], b3[:, pair, :], b4[:, pair, :], ALU.max)
-
         gate = tile("gate", [P, PACK, O], F32)
+
+        for t in range(PACK):
+            cols = slice(P * t, P * (t + 1))
+            bank = ps.tile([P, J], F32, name="b_bank%d" % t)
+            nc.tensor.matmul_mx(
+                bank[:], lhsT=w2_codes[:, cols].bitcast(E2M1), lhsT_scale=w2_sc[:, cols],
+                rhs=xo_codes[:].bitcast(E4M3), rhs_scale=xo_sc[:], start=True, stop=True,
+            )
+            rows = tile("b_rows%d" % t, [P, J], F32)
+            (nc.scalar.copy if t >= 2 else nc.vector.tensor_copy)(rows[:], bank[:])
+            nc.vector.tensor_copy(b3[:, t, :], rows[:].indirect(list3[:]))
+            nc.vector.tensor_copy(b4[:, t, :], rows[:].indirect(list4[:]))
+        nc.vector.tensor_tensor(top[:], b3[:], b4[:], ALU.max)
+
+        a_rows = []
+
+        def look(t):
+            nc.scalar.activation(gate[:, t, :], a_rows[t][:].indirect(list4[:]), ACT.Sigmoid, scale=slope[:, t : t + 1])
+
         for t in range(PACK):
             cols = slice(P * t, P * (t + 1))
             bank = ps.tile([P, J], F32, name="a_bank%d" % t)
@@ -131,19 +139,27 @@ def tile_list_twotab_agree_one_tabled_kernel(
                 rhs=xt_codes[:].bitcast(E2M1), rhs_scale=xt_sc[:], start=True, stop=True,
             )
             rows = tile("a_rows%d" % t, [P, J], F32)
-            nc.vector.tensor_copy(rows[:], bank[:])
-            nc.scalar.activation(gate[:, t, :], rows[:].indirect(list4[:]), ACT.Sigmoid, scale=slope[:, t : t + 1])
+            nc.scalar.copy(rows[:], bank[:])
+            a_rows.append(rows)
+            if t:
+                look(t - 1)
+        look(PACK - 1)
 
         hid = tile("hid", [P, O, PACK], BF16)
-        nc.vector.tensor_tensor(
-            hid[:].rearrange("p (c i) t -> p c t i", i=4),
-            top[:].rearrange("p t (c i) -> p c t i", i=4),
-            gate[:].rearrange("p t (c i) -> p c t i", i=4),
-            ALU.mult,
-        )
         hid_codes = tile("hid_codes", [P, O], U32)
         hid_sc = tile("hid_sc", [P, O], U8)
-        nc.vector.quantize_mx(hid_codes[:].bitcast(E5M2), hid_sc[:], hid[:].rearrange("p o t -> p (o t)"))
+        halves = (slice(0, O // 2), slice(O // 2, O))
+        for half in halves:
+            nc.vector.tensor_tensor(
+                hid[:, half, :].rearrange("p (c i) t -> p c t i", i=4),
+                top[:, :, half].rearrange("p t (c i) -> p c t i", i=4),
+                gate[:, :, half].rearrange("p t (c i) -> p c t i", i=4),
+                ALU.mult,
+            )
+        for half in halves:
+            nc.vector.quantize_mx(
+                hid_codes[:, half].bitcast(E5M2), hid_sc[:, half], hid[:, half, :].rearrange("p o t -> p (o t)")
+            )
 
         tz_picked = tile("tz_picked", [P, 2, O], F32, tag="a_rows3")
         res = tile("res", [P, 2, O], F32)
@@ -151,7 +167,7 @@ def tile_list_twotab_agree_one_tabled_kernel(
             nc.scalar.activation(tz_picked[:, h, :], tz_tab[:, h, :].indirect(list5[:]), ACT.Copy)
         for h, queue in enumerate((nc.sync, nc.scalar)):
             cols = slice(P * h, P * (h + 1))
-            bank = ps.tile([P, O], F32, name="p_bank%d" % h)
+            bank = ps.tile([P, O], F32, name="p_bank%d" % h, tag="b_bank%d" % h)
             nc.tensor.matmul_mx(
                 bank[:], lhsT=wb_codes[:, cols].bitcast(E2M1), lhsT_scale=wb_plane[:, cols],
                 rhs=hid_codes[:].bitcast(E5M2), rhs_scale=hid_sc[:], start=True, stop=True,

@@ -58,16 +58,14 @@ def tile_list_twotab_agree_one_tabled_kernel(
         xt_tab = tile("xt_tab", [P, T], U16)
         w_raw = tile("w_raw", [P, R], U32)
         w2_raw = tile("w2_raw", [P, R], U16)
-        wb_codes = tile("wb_codes", [P, N], U16)
-        slope = tile("slope", [P, PACK], F32)
 
-        xo_rows = load_rows(nc.scalar, "xo_rows", xo_scales)
-        list2 = load_list("list2", offs2)
         w2_rows = load_rows(nc.scalar, "w2_rows", w2_scales)
+        list2 = load_list("list2", offs2)
+        xo_rows = load_rows(nc.scalar, "xo_rows", xo_scales)
         list1 = load_list("list1", offs)
         xt_rows = load_rows(nc.scalar, "xt_rows", xt_scales)
+        w_rows = load_rows(nc.sync, "w_rows", w_scales)
         list3 = load_list("list3", offs3)
-        w_rows = load_rows(nc.scalar, "w_rows", w_scales)
         nc.sync.dma_start(xo_tab[:].bitcast(I32), xo_words[0].rearrange("p n t -> p (n t)").bitcast(I32))
         list4 = load_list("list4", offs4)
         list5 = load_list("list5", offs5)
@@ -75,8 +73,6 @@ def tile_list_twotab_agree_one_tabled_kernel(
         nc.sync.dma_start(xt_tab[:].bitcast(I32), xt_words[0].bitcast(I32))
         nc.sync.dma_start(w_raw[:].bitcast(I32), w_words[0].rearrange("p n t -> p (n t)").bitcast(I32))
         nc.gpsimd.dma_start(wb_plane[0:P:8, :].bitcast(I32), wb_scales[0].bitcast(I32))
-        nc.gpsimd.dma_start(slope[:], sg.rearrange("(p t) o -> p (t o)", t=PACK))
-        nc.gpsimd.dma_start(wb_codes[:].bitcast(I32), wb_words[0].bitcast(I32))
         warm = tile("warm", [P, 2], F32)
         nc.vector.memset(warm[:, 0:1], 0.0)
         nc.scalar.activation(warm[:, 1:2], warm[:, 0:1], ACT.Sigmoid)
@@ -84,17 +80,22 @@ def tile_list_twotab_agree_one_tabled_kernel(
         def deal(copy, dst, src):
             copy(dst[:].rearrange("p (t m) -> p m t", t=PACK), src[:].rearrange("p (m t) -> p m t", t=PACK))
 
+        def deal_bytes(dst, src):
+            nc.gpsimd.tensor_copy(dst.rearrange("p (t m) -> p t m", t=PACK), src[:].rearrange("p (m t) -> p t m", t=PACK))
+
         xo_picked = tile("xo_picked", [P, J], U8)
         nc.vector.tensor_copy(xo_picked[:], xo_rows[:].indirect(list2[:]))
-        deal(nc.vector.tensor_copy, w2_sc, w2_rows)
+        deal_bytes(w2_sc, w2_rows)
         nc.vector.tensor_copy(xo_sc.bitcast(I32), xo_picked[:].bitcast(I32))
         compact(b_planes)
 
         xt_picked = tile("xt_picked", [P, J], U8)
         nc.vector.tensor_copy(xt_picked[:], xt_rows[:].indirect(list1[:]))
-        deal(nc.vector.tensor_copy, w_sc, w_rows)
+        deal_bytes(w_sc, w_rows)
         nc.vector.tensor_copy(xt_sc.bitcast(I32), xt_picked[:].bitcast(I32))
         compact(a_planes)
+        slope = tile("slope", [P, PACK], F32, tag="xt_picked")
+        nc.sync.dma_start(slope[:], sg.rearrange("(p t) o -> p (t o)", t=PACK))
 
         xo_codes = tile("xo_codes", [P, J], U32)
         nc.vector.tensor_copy(xo_codes[:], xo_tab[:].indirect(list2[:]))
@@ -105,6 +106,8 @@ def tile_list_twotab_agree_one_tabled_kernel(
         w_codes = tile("w_codes", [P, R], U32)
         deal(nc.scalar.copy, w_codes, w_raw)
 
+        wb_codes = tile("wb_codes", [P, N], U16, tag="w_raw")
+        nc.sync.dma_start(wb_codes[:].bitcast(I32), wb_words[0].bitcast(I32))
         tz_tab = tile("tz_tab", [P, 2, E], F32, tag="xt_tab")
         nc.sync.dma_start(tz_tab[:], tz.rearrange("(h p) e -> p h e", p=P))
 
@@ -121,10 +124,12 @@ def tile_list_twotab_agree_one_tabled_kernel(
                 rhs=xo_codes[:].bitcast(E4M3), rhs_scale=xo_sc[:], start=True, stop=True,
             )
             rows = tile("b_rows%d" % t, [P, J], F32)
-            (nc.scalar.copy if t >= 2 else nc.vector.tensor_copy)(rows[:], bank[:])
+            (nc.scalar.copy if t else nc.vector.tensor_copy)(rows[:], bank[:])
             nc.vector.tensor_copy(b3[:, t, :], rows[:].indirect(list3[:]))
             nc.vector.tensor_copy(b4[:, t, :], rows[:].indirect(list4[:]))
-        nc.vector.tensor_tensor(top[:], b3[:], b4[:], ALU.max)
+            if t % 2:
+                pair = slice(t - 1, t + 1)
+                nc.vector.tensor_tensor(top[:, pair, :], b3[:, pair, :], b4[:, pair, :], ALU.max)
 
         a_rows = []
 

from contextlib import ExitStack

import concourse.mybir as mybir

F32 = mybir.dt.float32
BF16 = mybir.dt.bfloat16
I32 = mybir.dt.int32
U32 = mybir.dt.uint32
U16 = mybir.dt.uint16
U8 = mybir.dt.uint8
E4M3 = mybir.dt.float8_e4m3fn_x4
E5M2 = mybir.dt.float8_e5m2_x4
E2M1 = mybir.dt.float4_e2m1fn_x4
ACT = mybir.ActivationFunctionType
ALU = mybir.AluOpType

P = 128
PACK = 4
T, Z, J, R, O, N, E = 1024, 1024, 256, 512, 128, 256, 1024
FLOPS = 2 * 512 * R * J * 2 + 2 * R * N * O


def tile_list_twotab_agree_one_tabled_kernel(
    tc, xt_words, xt_scales, w_words, w_scales, xo_words, xo_scales, w2_words, w2_scales,
    sg, wb_words, wb_scales, tz, offs, offs2, offs3, offs4, offs5, out,
):
    nc = tc.nc
    with ExitStack() as ctx:
        sb = ctx.enter_context(tc.tile_pool(name="sb", bufs=1))
        ps = ctx.enter_context(tc.psum_pool(name="ps", bufs=1))

        def tile(name, shape, dtype, tag=""):
            return sb.tile(shape, dtype, name=name, tag=tag or name, align_bytes=64)

        def load_list(name, src):
            dst = tile(name, list(src.shape), U16)
            nc.sync.dma_start(dst[:], src)
            return dst

        def load_rows(queue, name, scales):
            rows = scales[0].bitcast(I32)
            words = rows.shape[1]
            dst = tile(name, [P, 4 * words], U8)
            queue.dma_start(dst[:].bitcast(I32), rows.unsqueeze(1).to_broadcast([16, 8, words]))
            return dst

        def compact(planes):
            words = planes[:].bitcast(I32)
            for r in range(1, PACK):
                nc.sync.dma_start(words[r:P:32, :], words[8 * r : P : 32, :])

        b_planes = tile("b_planes", [P, R + J], U8)
        a_planes = tile("a_planes", [P, R + J + N], U8)
        w2_sc, xo_sc = b_planes[:, 0:R], b_planes[:, R : R + J]
        w_sc, xt_sc, wb_plane = a_planes[:, 0:R], a_planes[:, R : R + J], a_planes[:, R + J :]

        xo_tab = tile("xo_tab", [P, Z], U32)
        xt_tab = tile("xt_tab", [P, T], U16)
        w_raw = tile("w_raw", [P, R], U32)
        w2_raw = tile("w2_raw", [P, R], U16)

        w2_rows = load_rows(nc.scalar, "w2_rows", w2_scales)
        list2 = load_list("list2", offs2)
        xo_rows = load_rows(nc.scalar, "xo_rows", xo_scales)
        list1 = load_list("list1", offs)
        xt_rows = load_rows(nc.scalar, "xt_rows", xt_scales)
        w_rows = load_rows(nc.sync, "w_rows", w_scales)
        list3 = load_list("list3", offs3)
        nc.sync.dma_start(xo_tab[:].bitcast(I32), xo_words[0].rearrange("p n t -> p (n t)").bitcast(I32))
        list4 = load_list("list4", offs4)
        list5 = load_list("list5", offs5)
        nc.sync.dma_start(w2_raw[:].bitcast(I32), w2_words[0].bitcast(I32))
        nc.sync.dma_start(xt_tab[:].bitcast(I32), xt_words[0].bitcast(I32))
        nc.sync.dma_start(w_raw[:].bitcast(I32), w_words[0].rearrange("p n t -> p (n t)").bitcast(I32))
        nc.gpsimd.dma_start(wb_plane[0:P:8, :].bitcast(I32), wb_scales[0].bitcast(I32))
        warm = tile("warm", [P, 2], F32)
        nc.vector.memset(warm[:, 0:1], 0.0)
        nc.scalar.activation(warm[:, 1:2], warm[:, 0:1], ACT.Sigmoid)

        def deal(copy, dst, src):
            copy(dst[:].rearrange("p (t m) -> p m t", t=PACK), src[:].rearrange("p (m t) -> p m t", t=PACK))

        def deal_bytes(dst, src):
            nc.gpsimd.tensor_copy(dst.rearrange("p (t m) -> p t m", t=PACK), src[:].rearrange("p (m t) -> p t m", t=PACK))

        xo_picked = tile("xo_picked", [P, J], U8)
        nc.vector.tensor_copy(xo_picked[:], xo_rows[:].indirect(list2[:]))
        deal_bytes(w2_sc, w2_rows)
        nc.vector.tensor_copy(xo_sc.bitcast(I32), xo_picked[:].bitcast(I32))
        compact(b_planes)

        xt_picked = tile("xt_picked", [P, J], U8)
        nc.vector.tensor_copy(xt_picked[:], xt_rows[:].indirect(list1[:]))
        deal_bytes(w_sc, w_rows)
        nc.vector.tensor_copy(xt_sc.bitcast(I32), xt_picked[:].bitcast(I32))
        compact(a_planes)
        slope = tile("slope", [P, PACK], F32, tag="xt_picked")
        nc.sync.dma_start(slope[:], sg.rearrange("(p t) o -> p (t o)", t=PACK))

        xo_codes = tile("xo_codes", [P, J], U32)
        nc.vector.tensor_copy(xo_codes[:], xo_tab[:].indirect(list2[:]))
        xt_codes = tile("xt_codes", [P, J], U16)
        nc.vector.tensor_copy(xt_codes[:], xt_tab[:].indirect(list1[:]))
        w2_codes = tile("w2_codes", [P, R], U16)
        deal(nc.scalar.copy, w2_codes, w2_raw)
        w_codes = tile("w_codes", [P, R], U32)
        deal(nc.scalar.copy, w_codes, w_raw)

        wb_codes = tile("wb_codes", [P, N], U16, tag="w_raw")
        nc.sync.dma_start(wb_codes[:].bitcast(I32), wb_words[0].bitcast(I32))
        tz_tab = tile("tz_tab", [P, 2, E], F32, tag="xt_tab")
        nc.sync.dma_start(tz_tab[:], tz.rearrange("(h p) e -> p h e", p=P))

        b3 = tile("b3", [P, PACK, O], F32)
        b4 = tile("b4", [P, PACK, O], F32)
        top = tile("top", [P, PACK, O], F32)
        gate = tile("gate", [P, PACK, O], F32)

        for t in range(PACK):
            cols = slice(P * t, P * (t + 1))
            bank = ps.tile([P, J], F32, name="b_bank%d" % t)
            nc.tensor.matmul_mx(
                bank[:], lhsT=w2_codes[:, cols].bitcast(E2M1), lhsT_scale=w2_sc[:, cols],
                rhs=xo_codes[:].bitcast(E4M3), rhs_scale=xo_sc[:], start=True, stop=True,
            )
            rows = tile("b_rows%d" % t, [P, J], F32)
            (nc.scalar.copy if t else nc.vector.tensor_copy)(rows[:], bank[:])
            nc.vector.tensor_copy(b3[:, t, :], rows[:].indirect(list3[:]))
            nc.vector.tensor_copy(b4[:, t, :], rows[:].indirect(list4[:]))
            if t % 2:
                pair = slice(t - 1, t + 1)
                nc.vector.tensor_tensor(top[:, pair, :], b3[:, pair, :], b4[:, pair, :], ALU.max)

        a_rows = []

        def look(t):
            nc.scalar.activation(gate[:, t, :], a_rows[t][:].indirect(list4[:]), ACT.Sigmoid, scale=slope[:, t : t + 1])

        for t in range(PACK):
            cols = slice(P * t, P * (t + 1))
            bank = ps.tile([P, J], F32, name="a_bank%d" % t)
            nc.tensor.matmul_mx(
                bank[:], lhsT=w_codes[:, cols].bitcast(E4M3), lhsT_scale=w_sc[:, cols],
                rhs=xt_codes[:].bitcast(E2M1), rhs_scale=xt_sc[:], start=True, stop=True,
            )
            rows = tile("a_rows%d" % t, [P, J], F32)
            nc.scalar.copy(rows[:], bank[:])
            a_rows.append(rows)
            if t:
                look(t - 1)
        look(PACK - 1)

        hid = tile("hid", [P, O, PACK], BF16)
        hid_codes = tile("hid_codes", [P, O], U32)
        hid_sc = tile("hid_sc", [P, O], U8)
        halves = (slice(0, O // 2), slice(O // 2, O))
        for half in halves:
            nc.vector.tensor_tensor(
                hid[:, half, :].rearrange("p (c i) t -> p c t i", i=4),
                top[:, :, half].rearrange("p t (c i) -> p c t i", i=4),
                gate[:, :, half].rearrange("p t (c i) -> p c t i", i=4),
                ALU.mult,
            )
        for half in halves:
            nc.vector.quantize_mx(
                hid_codes[:, half].bitcast(E5M2), hid_sc[:, half], hid[:, half, :].rearrange("p o t -> p (o t)")
            )

        tz_picked = tile("tz_picked", [P, 2, O], F32, tag="a_rows3")
        res = tile("res", [P, 2, O], F32)
        for h in range(2):
            nc.scalar.activation(tz_picked[:, h, :], tz_tab[:, h, :].indirect(list5[:]), ACT.Copy)
        for h, queue in enumerate((nc.sync, nc.scalar)):
            cols = slice(P * h, P * (h + 1))
            bank = ps.tile([P, O], F32, name="p_bank%d" % h, tag="b_bank%d" % h)
            nc.tensor.matmul_mx(
                bank[:], lhsT=wb_codes[:, cols].bitcast(E2M1), lhsT_scale=wb_plane[:, cols],
                rhs=hid_codes[:].bitcast(E5M2), rhs_scale=hid_sc[:], start=True, stop=True,
            )
            nc.vector.tensor_tensor(res[:, h, :], bank[:], tz_picked[:, h, :], ALU.add)
            queue.dma_start(out[cols, :], res[:, h, :])
